import numpy as np
import ml_dtypes


def mxq(x, axis, fmt="e4m3"):
    dtype, down = {"e4m3": (ml_dtypes.float8_e4m3fn, 7), "e5m2": (ml_dtypes.float8_e5m2, 14)}[fmt]
    v = np.moveaxis(np.asarray(x, np.float32).astype(ml_dtypes.bfloat16).astype(np.float64), axis, -1)
    blocks = v.reshape(v.shape[:-1] + (-1, 32))
    amax = np.abs(blocks).max(-1, keepdims=True)
    byte = np.maximum(np.where(amax > 0, np.frexp(amax)[1] - 1 + 127, 0) - down, 1)
    scale = np.exp2(byte - 127.0)
    codes = (blocks / scale).astype(np.float32).astype(dtype).astype(np.float64)
    return np.moveaxis((codes * scale).reshape(v.shape), -1, axis)


WIDE = False


def mx_kscale(k):
    if not WIDE:
        return np.ones(k)
    levels = np.array([30, -30])
    if k % 512:
        return np.exp2(np.random.permutation(np.resize(levels, k // 32))).repeat(32)
    a = np.empty((k // 512, 16))
    for p in range(k // 512):
        a[p, :8] = np.random.permutation(np.resize(levels, 8))
        for g in range(8):
            far = levels[np.abs(levels - a[p, g]) >= 10]
            a[p, g + 8] = far[np.random.randint(len(far))]
    return np.exp2(a.ravel()).repeat(32)


def f64(x):
    return np.asarray(x).astype(np.float64)


def striped(idx):
    return np.tile(np.asarray(idx).reshape(-1, 16).T, (8, 1)).astype(np.uint16)


def unstriped(offs):
    return offs[:16].T.reshape(-1).astype(np.int64)


K, J, N, T, V = 256, 1024, 256, 2048, 2048


def setup_inputs():
    n = np.random.standard_normal
    idx = np.random.permutation(T)[:J]
    idx2 = np.random.permutation(V)[:J]
    fj = mx_kscale(J)
    return {
        "xf": (n((K, T))).astype(np.float32),
        "ra": (np.random.uniform(0.5, 1.5, (1, J)) * fj).astype(np.float32),
        "gt": (n((N, V)) * np.exp(0.5 * n((1, V)))).astype(np.float32),
        "cb": (np.random.uniform(0.5, 1.5, (J, 1)) / fj[:, None]).astype(np.float32),
        "bn": (np.random.uniform(-0.5, 0.5, (1, N))).astype(np.float32),
        "offs": striped(idx),
        "offs2": striped(idx2),
    }


def reference(xf, ra, gt, cb, bn, offs, offs2):
    idx = unstriped(offs)
    idx2 = unstriped(offs2)
    xg = f64(xf)[:, idx]
    x1 = np.pad(xg, ((0, 0), (1, 0)))[:, :J]
    us = (xg - 0.6 * x1) * f64(ra)
    uj = us.T
    gr1 = f64(gt)[:, idx2].T
    gj = gr1 / (np.max(np.abs(gr1), axis=1, keepdims=True) + 0.2) * f64(cb)
    ujq = mxq(uj, 0, "e4m3")
    gjq = mxq(gj, 0, "e5m2")
    w = ujq.T @ gjq
    ew = np.exp(0.02 * w + f64(bn))
    y = 256.0 * ew / np.sum(ew, axis=1, keepdims=True)
    return y

@@ -1,0 +1,208 @@
+from contextlib import ExitStack
+
+import concourse.mybir as mybir
+from concourse.masks import make_identity
+
+K, J, N, T, V = 256, 1024, 256, 2048, 2048
+FLOPS = 2 * K * J * N
+
+F32 = mybir.dt.float32
+BF16 = mybir.dt.bfloat16
+U32 = mybir.dt.uint32
+U16 = mybir.dt.uint16
+U8 = mybir.dt.uint8
+E4M3 = mybir.dt.float8_e4m3fn_x4
+E5M2 = mybir.dt.float8_e5m2_x4
+ALU = mybir.AluOpType
+ACT = mybir.ActivationFunctionType
+AX = mybir.AxisListType
+
+P = 128
+PACK = 4
+PASS = P * PACK
+PASSES = J // PASS
+COLS = PASS // 16
+PAD = 8
+
+
+def tile_list_moment_steps_sized_shares_kernel(tc, xf, ra, gt, cb, bn, offs, offs2, out):
+    nc = tc.nc
+    with ExitStack() as ctx:
+        keep = ctx.enter_context(tc.tile_pool(name="keep", bufs=1))
+        psum = ctx.enter_context(tc.psum_pool(name="psum", bufs=1))
+
+        x_list = keep.tile([P, J // 16], U16, name="x_list")
+        g_list = keep.tile([P, J // 16], U16, name="g_list")
+        g_win = [keep.tile([P, V], F32, name=f"g_win{h}", tag=f"g_win{h}") for h in range(2)]
+        x_win = [keep.tile([P, T], F32, name=f"x_win{h}") for h in range(2)]
+        ra_t = keep.tile([P, PASSES, 2 * PACK], F32, name="ra_t")
+        cb_t = keep.tile([P, PASSES, 2 * PACK], F32, name="cb_t")
+        bn_col = keep.tile([P, 2], F32, name="bn_col")
+
+        nc.sync.dma_start(g_list[:], offs2)
+        nc.sync.dma_start(g_win[0][:], gt[0:P, :])
+        nc.scalar.dma_start(bn_col[:], bn.rearrange("o (p e) -> p (o e)", e=2))
+        nc.scalar.dma_start(cb_t[:, :, 0:PACK], cb.rearrange("(a p t) o -> p a (t o)", p=P, t=PACK))
+        nc.scalar.dma_start(ra_t[:, :, 0:PACK], ra.rearrange("o (a p t) -> p (o a) t", p=P, t=PACK))
+        nc.sync.dma_start(g_win[1][:], gt[P : 2 * P, :])
+        nc.sync.dma_start(x_list[:], offs)
+        nc.sync.dma_start(x_win[0][:], xf[0:P, :])
+        nc.sync.dma_start(x_win[1][:], xf[P : 2 * P, :])
+
+        ident = keep.tile([P, P], F32, name="ident")
+        make_identity(nc, ident[:])
+
+        bn_bank = psum.tile([P, 2, P], F32, name="bn_bank", tag="w")
+        for e in range(2):
+            nc.tensor.transpose(bn_bank[:, e, :], bn_col[:, e : e + 1].to_broadcast([P, P]), ident[:])
+        bn_rows = keep.tile([P, N], F32, name="bn_rows")
+        nc.scalar.activation(bn_rows[:].rearrange("m (p e) -> m p e", e=2), bn_bank[:].rearrange("m e p -> m p e"), ACT.Copy)
+
+        x_run = [keep.tile([P, PAD + J], F32, name=f"x_run{h}") for h in range(2)]
+        zero = keep.tile([P, 1], F32, name="zero")
+        nc.vector.memset(zero[:], 0.0)
+        for h in range(2):
+            nc.scalar.activation(x_run[h][:, PAD - 1 : PAD], zero[:], ACT.Copy)
+
+        g_bank = {}
+        g_peak = {}
+        first_turned = []
+
+        def g_gather_turn(h, a):
+            picked = keep.tile([P, PASS], F32, name=f"g_pick{h}{a}")
+            window = g_win[h][:].indirect(g_list[:, a * COLS : (a + 1) * COLS])
+            bank = psum.tile([P, PACK, P], F32, name=f"g_bank{h}{a}")
+            if (h, a) in ((0, 0), (1, 0)):
+                nc.vector.tensor_copy(picked[:].rearrange("p (t q) -> p q t", t=PACK), window)
+                for t in range(PACK):
+                    nc.tensor.transpose(bank[:, t, :], picked[:, t * P : (t + 1) * P], ident[:])
+            else:
+                nc.scalar.activation(picked[:], window, ACT.Copy)
+                for t in range(PACK):
+                    nc.tensor.transpose(bank[:, t, :], picked[:, t:PASS:PACK], ident[:])
+            g_bank[h, a] = bank
+
+        def g_measure(h, a):
+            if h == 0:
+                if not first_turned:
+                    first_turned.append(keep.tile([P, PASSES, PACK, P], F32, name="g_turn0", tag="g_win1"))
+                turned = first_turned[0][:, a]
+            else:
+                turned = keep.tile([P, PACK, P], F32, name=f"g_turn{h}{a}")[:]
+            nc.scalar.copy(turned, g_bank[h, a][:])
+            peak = keep.tile([P, PACK], F32, name=f"g_peak{h}{a}")
+            nc.vector.tensor_reduce(peak[:], turned, AX.X, ALU.max, apply_absolute_value=True)
+            if h == 0:
+                nc.vector.tensor_scalar_add(peak[:], peak[:], 0.2)
+            g_peak[h, a] = peak
+
+        g_codes = {}
+        g_scales = {}
+
+        def g_finish(a):
+            den = keep.tile([P, PACK], F32, name=f"den{a}")
+            nc.vector.scalar_tensor_tensor(den[:], g_peak[1, a][:], 0.2, g_peak[0, a][:], ALU.add, ALU.max)
+            inv = keep.tile([P, PACK], F32, name=f"inv{a}")
+            nc.vector.reciprocal(inv[:], den[:])
+            factor = keep.tile([P, PACK], F32, name=f"factor{a}")
+            nc.vector.tensor_tensor(factor[:], inv[:], cb_t[:, a, 0:PACK], ALU.mult)
+            woven = keep.tile([P, N, PACK], BF16, name=f"g_woven{a}", align_bytes=64)
+            for h in range(2):
+                nc.vector.tensor_tensor(
+                    woven[:, h * P : (h + 1) * P, :],
+                    g_bank[h, a][:].rearrange("p t n -> p n t"),
+                    factor[:].unsqueeze(1).to_broadcast([P, P, PACK]),
+                    ALU.mult,
+                )
+            g_codes[a] = keep.tile([P, N], U32, name=f"g_codes{a}", align_bytes=64)
+            g_scales[a] = keep.tile([P, N], U8, name=f"g_scales{a}", align_bytes=64)
+            nc.vector.quantize_mx(g_codes[a][:].bitcast(E5M2), g_scales[a][:], woven[:].rearrange("p n t -> p (n t)"))
+
+        u_codes = {}
+        u_scales = {}
+        x_bank = {}
+
+        def x_gather_turn(h, a):
+            lo = PAD + a * PASS
+            run = x_run[h]
+            nc.scalar.activation(run[:, lo : lo + PASS], x_win[h][:].indirect(x_list[:, a * COLS : (a + 1) * COLS]), ACT.Copy)
+            step = keep.tile([P, PACK, P], F32, name=f"x_step{h}{a}")
+            bank = psum.tile([P, PACK, P], F32, name=f"x_bank{h}{a}", tag="x_bank", bufs=3)
+            if (h, a) in ((0, 0), (0, 1), (1, 0)):
+                nc.gpsimd.tensor_scalar(
+                    step[:], run[:, lo - 1 : lo - 1 + PASS].rearrange("p (q t) -> p t q", t=PACK), -0.6, 0.0, ALU.mult, ALU.add
+                )
+                for t in range(PACK):
+                    nc.tensor.matmul(bank[:, t, :], run[:, lo + t : lo + PASS : PACK], ident[:], start=(t == 0), stop=False, is_transpose=True)
+                for t in range(PACK):
+                    nc.tensor.matmul(bank[:, t, :], step[:, t, :], ident[:], start=False, stop=(t == PACK - 1), is_transpose=True)
+            else:
+                nc.vector.scalar_tensor_tensor(
+                    step[:].rearrange("p t q -> p q t"),
+                    run[:, lo - 1 : lo - 1 + PASS].rearrange("p (q t) -> p q t", t=PACK),
+                    -0.6,
+                    run[:, lo : lo + PASS].rearrange("p (q t) -> p q t", t=PACK),
+                    ALU.mult,
+                    ALU.add,
+                )
+                for t in range(PACK):
+                    nc.tensor.transpose(bank[:, t, :], step[:, t, :], ident[:])
+            x_bank[h, a] = bank
+
+        def x_finish(h, a):
+            woven = keep.tile([P, P, PACK], BF16, name=f"u_woven{h}{a}", align_bytes=64)
+            nc.vector.tensor_tensor(
+                woven[:],
+                x_bank[h, a][:].rearrange("p t k -> p k t"),
+                ra_t[:, a, 0:PACK].unsqueeze(1).to_broadcast([P, P, PACK]),
+                ALU.mult,
+            )
+            u_codes[h, a] = keep.tile([P, P], U32, name=f"u_codes{h}{a}", align_bytes=64)
+            u_scales[h, a] = keep.tile([P, P], U8, name=f"u_scales{h}{a}", align_bytes=64)
+            nc.vector.quantize_mx(u_codes[h, a][:].bitcast(E4M3), u_scales[h, a][:], woven[:].rearrange("p k t -> p (k t)"))
+
+        def shares(h):
+            moment = psum.tile([P, N], F32, name=f"moment{h}", tag="w")
+            for a in range(PASSES):
+                nc.tensor.matmul_mx(
+                    out=moment[:],
+                    lhsT=u_codes[h, a][:].bitcast(E4M3),
+                    lhsT_scale=u_scales[h, a][:],
+                    rhs=g_codes[a][:].bitcast(E5M2),
+                    rhs_scale=g_scales[a][:],
+                    start=(a == 0),
+                    stop=(a == PASSES - 1),
+                )
+            minus_z = keep.tile([P, N], F32, name=f"minus_z{h}")
+            nc.vector.scalar_tensor_tensor(minus_z[:], moment[:], -0.02, bn_rows[:], ALU.mult, ALU.subtract)
+            low = keep.tile([P, 1], F32, name=f"low{h}")
+            nc.vector.tensor_reduce(low[:], minus_z[:], AX.X, ALU.min)
+            ew = keep.tile([P, N], F32, name=f"ew{h}")
+            total = keep.tile([P, 1], F32, name=f"total{h}")
+            nc.scalar.activation(ew[:], minus_z[:], ACT.Exp, bias=low[:], scale=-1.0, accum_out=total[:])
+            inv_total = keep.tile([P, 1], F32, name=f"inv_total{h}")
+            nc.vector.reciprocal(inv_total[:], total[:])
+            result = keep.tile([P, N], F32, name=f"result{h}")
+            nc.vector.tensor_scalar(result[:], ew[:], inv_total[:], 256.0, ALU.mult, ALU.mult)
+            nc.sync.dma_start(out[h * P : (h + 1) * P, :], result[:])
+
+        g_gather_turn(0, 0)
+        g_gather_turn(0, 1)
+        g_gather_turn(1, 0)
+        g_gather_turn(1, 1)
+        g_measure(0, 0)
+        g_measure(0, 1)
+        g_measure(1, 0)
+        g_finish(0)
+        g_measure(1, 1)
+        g_finish(1)
+        x_gather_turn(0, 0)
+        x_gather_turn(0, 1)
+        x_finish(0, 0)
+        x_finish(0, 1)
+        x_gather_turn(1, 0)
+        x_gather_turn(1, 1)
+        x_finish(1, 0)
+        shares(0)
+        x_finish(1, 1)
+        shares(1)

@@ -19,6 +19,7 @@ AX = mybir.AxisListType
 
 P = 128
 PACK = 4
+RUN = 8
 PASS = P * PACK
 PASSES = J // PASS
 COLS = PASS // 16
@@ -35,34 +36,49 @@ def tile_list_moment_steps_sized_shares_kernel(tc, xf, ra, gt, cb, bn, offs, off
         g_list = keep.tile([P, J // 16], U16, name="g_list")
         g_win = [keep.tile([P, V], F32, name=f"g_win{h}", tag=f"g_win{h}") for h in range(2)]
         x_win = [keep.tile([P, T], F32, name=f"x_win{h}") for h in range(2)]
-        ra_t = keep.tile([P, PASSES, 2 * PACK], F32, name="ra_t")
-        cb_t = keep.tile([P, PASSES, 2 * PACK], F32, name="cb_t")
+        ra_0 = keep.tile([P, PACK], F32, name="ra_0")
+        cb_0 = keep.tile([P, PACK], F32, name="cb_0")
         bn_col = keep.tile([P, 2], F32, name="bn_col")
+        rows_1 = keep.tile([P, P], F32, name="rows_1")
+        nc.vector.memset(rows_1[:], 0.0)
 
         nc.sync.dma_start(g_list[:], offs2)
         nc.sync.dma_start(g_win[0][:], gt[0:P, :])
         nc.scalar.dma_start(bn_col[:], bn.rearrange("o (p e) -> p (o e)", e=2))
-        nc.scalar.dma_start(cb_t[:, :, 0:PACK], cb.rearrange("(a p t) o -> p a (t o)", p=P, t=PACK))
-        nc.scalar.dma_start(ra_t[:, :, 0:PACK], ra.rearrange("o (a p t) -> p (o a) t", p=P, t=PACK))
+        nc.scalar.dma_start(
+            rows_1[0:PACK, :].rearrange("t (b r) -> t b r", r=RUN),
+            ra[:, PASS:J].rearrange("o (b t r) -> t (o b) r", t=PACK, r=RUN),
+        )
+        nc.scalar.dma_start(
+            rows_1[PACK : 2 * PACK, :].rearrange("t (b r) -> t b r", r=RUN),
+            cb[PASS:J, :].rearrange("(b t r) o -> t b (r o)", t=PACK, r=RUN),
+        )
         nc.sync.dma_start(g_win[1][:], gt[P : 2 * P, :])
         nc.sync.dma_start(x_list[:], offs)
+        nc.sync.dma_start(cb_0[:], cb[0:PASS, :].rearrange("(p t) o -> p (t o)", t=PACK))
+        nc.sync.dma_start(ra_0[:], ra[:, 0:PASS].rearrange("o (p t) -> p (o t)", t=PACK))
         nc.sync.dma_start(x_win[0][:], xf[0:P, :])
         nc.sync.dma_start(x_win[1][:], xf[P : 2 * P, :])
 
         ident = keep.tile([P, P], F32, name="ident")
         make_identity(nc, ident[:])
 
-        bn_bank = psum.tile([P, 2, P], F32, name="bn_bank", tag="w")
-        for e in range(2):
-            nc.tensor.transpose(bn_bank[:, e, :], bn_col[:, e : e + 1].to_broadcast([P, P]), ident[:])
-        bn_rows = keep.tile([P, N], F32, name="bn_rows")
-        nc.scalar.activation(bn_rows[:].rearrange("m (p e) -> m p e", e=2), bn_bank[:].rearrange("m e p -> m p e"), ACT.Copy)
-
         x_run = [keep.tile([P, PAD + J], F32, name=f"x_run{h}") for h in range(2)]
         zero = keep.tile([P, 1], F32, name="zero")
         nc.vector.memset(zero[:], 0.0)
         for h in range(2):
             nc.scalar.activation(x_run[h][:, PAD - 1 : PAD], zero[:], ACT.Copy)
+
+        head_bank = psum.tile([P, 3, P], F32, name="head_bank", tag="w")
+        for e in range(2):
+            nc.tensor.transpose(head_bank[:, e, :], bn_col[:, e : e + 1].to_broadcast([P, P]), ident[:])
+        nc.tensor.transpose(head_bank[:, 2, :], rows_1[:], ident[:])
+        bn_rows = keep.tile([P, N], F32, name="bn_rows")
+        nc.scalar.copy(bn_rows[:].rearrange("m (p e) -> m p e", e=2), head_bank[:, 0:2, :].rearrange("m e p -> m p e"))
+        weights_1 = keep.tile([P, 2 * PACK], F32, name="weights_1")
+        nc.scalar.copy(weights_1[:], head_bank[:, 2, 0 : 2 * PACK])
+        ra_w = [ra_0[:], weights_1[:, 0:PACK]]
+        cb_w = [cb_0[:], weights_1[:, PACK : 2 * PACK]]
 
         g_bank = {}
         g_peak = {}
@@ -72,8 +88,8 @@ def tile_list_moment_steps_sized_shares_kernel(tc, xf, ra, gt, cb, bn, offs, off
             picked = keep.tile([P, PASS], F32, name=f"g_pick{h}{a}")
             window = g_win[h][:].indirect(g_list[:, a * COLS : (a + 1) * COLS])
             bank = psum.tile([P, PACK, P], F32, name=f"g_bank{h}{a}")
-            if (h, a) in ((0, 0), (1, 0)):
-                nc.vector.tensor_copy(picked[:].rearrange("p (t q) -> p q t", t=PACK), window)
+            if a == 1:
+                nc.vector.tensor_copy(picked[:].rearrange("p (t b r) -> p b t r", t=PACK, r=RUN), window)
                 for t in range(PACK):
                     nc.tensor.transpose(bank[:, t, :], picked[:, t * P : (t + 1) * P], ident[:])
             else:
@@ -105,8 +121,8 @@ def tile_list_moment_steps_sized_shares_kernel(tc, xf, ra, gt, cb, bn, offs, off
             inv = keep.tile([P, PACK], F32, name=f"inv{a}")
             nc.vector.reciprocal(inv[:], den[:])
             factor = keep.tile([P, PACK], F32, name=f"factor{a}")
-            nc.vector.tensor_tensor(factor[:], inv[:], cb_t[:, a, 0:PACK], ALU.mult)
-            woven = keep.tile([P, N, PACK], BF16, name=f"g_woven{a}", align_bytes=64)
+            nc.vector.tensor_tensor(factor[:], inv[:], cb_w[a], ALU.mult)
+            woven = keep.tile([P, N, PACK], BF16, name=f"g_woven{a}", tag=f"stage{a}", align_bytes=64)
             for h in range(2):
                 nc.vector.tensor_tensor(
                     woven[:, h * P : (h + 1) * P, :],
@@ -126,9 +142,9 @@ def tile_list_moment_steps_sized_shares_kernel(tc, xf, ra, gt, cb, bn, offs, off
             lo = PAD + a * PASS
             run = x_run[h]
             nc.scalar.activation(run[:, lo : lo + PASS], x_win[h][:].indirect(x_list[:, a * COLS : (a + 1) * COLS]), ACT.Copy)
-            step = keep.tile([P, PACK, P], F32, name=f"x_step{h}{a}")
+            step = keep.tile([P, PACK, P], F32, name=f"x_step{h}{a}", tag=f"stage{1 - h}" if a == 1 else f"x_step{h}", align_bytes=64)
             bank = psum.tile([P, PACK, P], F32, name=f"x_bank{h}{a}", tag="x_bank", bufs=3)
-            if (h, a) in ((0, 0), (0, 1), (1, 0)):
+            if a == 0:
                 nc.gpsimd.tensor_scalar(
                     step[:], run[:, lo - 1 : lo - 1 + PASS].rearrange("p (q t) -> p t q", t=PACK), -0.6, 0.0, ALU.mult, ALU.add
                 )
@@ -137,15 +153,12 @@ def tile_list_moment_steps_sized_shares_kernel(tc, xf, ra, gt, cb, bn, offs, off
                 for t in range(PACK):
                     nc.tensor.matmul(bank[:, t, :], step[:, t, :], ident[:], start=False, stop=(t == PACK - 1), is_transpose=True)
             else:
-                nc.vector.scalar_tensor_tensor(
-                    step[:].rearrange("p t q -> p q t"),
-                    run[:, lo - 1 : lo - 1 + PASS].rearrange("p (q t) -> p q t", t=PACK),
-                    -0.6,
-                    run[:, lo : lo + PASS].rearrange("p (q t) -> p q t", t=PACK),
-                    ALU.mult,
-                    ALU.add,
-                )
+                before = run[:, lo - 1 : lo - 1 + PASS].rearrange("p (b t r) -> p t b r", t=PACK, r=RUN)
+                here = run[:, lo : lo + PASS].rearrange("p (b t r) -> p t b r", t=PACK, r=RUN)
                 for t in range(PACK):
+                    nc.vector.scalar_tensor_tensor(
+                        step[:, t, :].rearrange("p (b r) -> p b r", r=RUN), before[:, t], -0.6, here[:, t], ALU.mult, ALU.add
+                    )
                     nc.tensor.transpose(bank[:, t, :], step[:, t, :], ident[:])
             x_bank[h, a] = bank
 
@@ -154,7 +167,7 @@ def tile_list_moment_steps_sized_shares_kernel(tc, xf, ra, gt, cb, bn, offs, off
             nc.vector.tensor_tensor(
                 woven[:],
                 x_bank[h, a][:].rearrange("p t k -> p k t"),
-                ra_t[:, a, 0:PACK].unsqueeze(1).to_broadcast([P, P, PACK]),
+                ra_w[a].unsqueeze(1).to_broadcast([P, P, PACK]),
                 ALU.mult,
             )
             u_codes[h, a] = keep.tile([P, P], U32, name=f"u_codes{h}{a}", align_bytes=64)
@@ -186,23 +199,23 @@ def tile_list_moment_steps_sized_shares_kernel(tc, xf, ra, gt, cb, bn, offs, off
             nc.vector.tensor_scalar(result[:], ew[:], inv_total[:], 256.0, ALU.mult, ALU.mult)
             nc.sync.dma_start(out[h * P : (h + 1) * P, :], result[:])
 
-        g_gather_turn(0, 0)
         g_gather_turn(0, 1)
-        g_gather_turn(1, 0)
+        g_gather_turn(0, 0)
         g_gather_turn(1, 1)
-        g_measure(0, 0)
+        g_gather_turn(1, 0)
         g_measure(0, 1)
-        g_measure(1, 0)
-        g_finish(0)
+        g_measure(0, 0)
         g_measure(1, 1)
         g_finish(1)
+        g_measure(1, 0)
+        g_finish(0)
         x_gather_turn(0, 0)
         x_gather_turn(0, 1)
         x_finish(0, 0)
-        x_finish(0, 1)
         x_gather_turn(1, 0)
         x_gather_turn(1, 1)
+        x_finish(0, 1)
         x_finish(1, 0)
-        shares(0)
         x_finish(1, 1)
+        shares(0)
         shares(1)

@@ -45,18 +45,18 @@ def tile_list_moment_steps_sized_shares_kernel(tc, xf, ra, gt, cb, bn, offs, off
         nc.sync.dma_start(g_list[:], offs2)
         nc.sync.dma_start(g_win[0][:], gt[0:P, :])
         nc.scalar.dma_start(bn_col[:], bn.rearrange("o (p e) -> p (o e)", e=2))
-        nc.scalar.dma_start(
-            rows_1[0:PACK, :].rearrange("t (b r) -> t b r", r=RUN),
-            ra[:, PASS:J].rearrange("o (b t r) -> t (o b) r", t=PACK, r=RUN),
-        )
-        nc.scalar.dma_start(
-            rows_1[PACK : 2 * PACK, :].rearrange("t (b r) -> t b r", r=RUN),
-            cb[PASS:J, :].rearrange("(b t r) o -> t b (r o)", t=PACK, r=RUN),
-        )
         nc.sync.dma_start(g_win[1][:], gt[P : 2 * P, :])
         nc.sync.dma_start(x_list[:], offs)
         nc.sync.dma_start(cb_0[:], cb[0:PASS, :].rearrange("(p t) o -> p (t o)", t=PACK))
         nc.sync.dma_start(ra_0[:], ra[:, 0:PASS].rearrange("o (p t) -> p (o t)", t=PACK))
+        nc.sync.dma_start(
+            rows_1[0:PACK, :].rearrange("t (b r) -> t b r", r=RUN),
+            ra[:, PASS:J].rearrange("o (b t r) -> t (o b) r", t=PACK, r=RUN),
+        )
+        nc.sync.dma_start(
+            rows_1[PACK : 2 * PACK, :].rearrange("t (b r) -> t b r", r=RUN),
+            cb[PASS:J, :].rearrange("(b t r) o -> t b (r o)", t=PACK, r=RUN),
+        )
         nc.sync.dma_start(x_win[0][:], xf[0:P, :])
         nc.sync.dma_start(x_win[1][:], xf[P : 2 * P, :])
 
@@ -69,16 +69,19 @@ def tile_list_moment_steps_sized_shares_kernel(tc, xf, ra, gt, cb, bn, offs, off
         for h in range(2):
             nc.scalar.activation(x_run[h][:, PAD - 1 : PAD], zero[:], ACT.Copy)
 
-        head_bank = psum.tile([P, 3, P], F32, name="head_bank", tag="w")
+        head_bank = psum.tile([P, 2, P], F32, name="head_bank", tag="w")
         for e in range(2):
             nc.tensor.transpose(head_bank[:, e, :], bn_col[:, e : e + 1].to_broadcast([P, P]), ident[:])
-        nc.tensor.transpose(head_bank[:, 2, :], rows_1[:], ident[:])
         bn_rows = keep.tile([P, N], F32, name="bn_rows")
-        nc.scalar.copy(bn_rows[:].rearrange("m (p e) -> m p e", e=2), head_bank[:, 0:2, :].rearrange("m e p -> m p e"))
+        nc.scalar.copy(bn_rows[:].rearrange("m (p e) -> m p e", e=2), head_bank[:].rearrange("m e p -> m p e"))
         weights_1 = keep.tile([P, 2 * PACK], F32, name="weights_1")
-        nc.scalar.copy(weights_1[:], head_bank[:, 2, 0 : 2 * PACK])
         ra_w = [ra_0[:], weights_1[:, 0:PACK]]
         cb_w = [cb_0[:], weights_1[:, PACK : 2 * PACK]]
+
+        def turn_weights():
+            bank = psum.tile([P, P], F32, name="weights_bank", tag="w")
+            nc.tensor.transpose(bank[:], rows_1[:], ident[:])
+            nc.vector.tensor_copy(weights_1[:], bank[:, 0 : 2 * PACK])
 
         g_bank = {}
         g_peak = {}
@@ -87,7 +90,7 @@ def tile_list_moment_steps_sized_shares_kernel(tc, xf, ra, gt, cb, bn, offs, off
         def g_gather_turn(h, a):
             picked = keep.tile([P, PASS], F32, name=f"g_pick{h}{a}")
             window = g_win[h][:].indirect(g_list[:, a * COLS : (a + 1) * COLS])
-            bank = psum.tile([P, PACK, P], F32, name=f"g_bank{h}{a}")
+            bank = psum.tile([P, PACK, P], F32, name=f"g_bank{h}{a}", tag=f"g_bank{h}{a}")
             if a == 1:
                 nc.vector.tensor_copy(picked[:].rearrange("p (t b r) -> p b t r", t=PACK, r=RUN), window)
                 for t in range(PACK):
@@ -115,14 +118,20 @@ def tile_list_moment_steps_sized_shares_kernel(tc, xf, ra, gt, cb, bn, offs, off
         g_codes = {}
         g_scales = {}
 
-        def g_finish(a):
+        g_factor = {}
+
+        def g_weigh(a):
             den = keep.tile([P, PACK], F32, name=f"den{a}")
             nc.vector.scalar_tensor_tensor(den[:], g_peak[1, a][:], 0.2, g_peak[0, a][:], ALU.add, ALU.max)
-            inv = keep.tile([P, PACK], F32, name=f"inv{a}")
+            inv = keep.tile([P, PACK], F32, name=f"inv{a}", tag=f"inv{a}")
             nc.vector.reciprocal(inv[:], den[:])
             factor = keep.tile([P, PACK], F32, name=f"factor{a}")
             nc.vector.tensor_tensor(factor[:], inv[:], cb_w[a], ALU.mult)
-            woven = keep.tile([P, N, PACK], BF16, name=f"g_woven{a}", tag=f"stage{a}", align_bytes=64)
+            g_factor[a] = factor
+
+        def g_finish(a):
+            factor = g_factor[a]
+            woven = keep.tile([P, N, PACK], BF16, name=f"g_woven{a}", tag=f"g_woven{a}", align_bytes=64)
             for h in range(2):
                 nc.vector.tensor_tensor(
                     woven[:, h * P : (h + 1) * P, :],
@@ -142,11 +151,19 @@ def tile_list_moment_steps_sized_shares_kernel(tc, xf, ra, gt, cb, bn, offs, off
             lo = PAD + a * PASS
             run = x_run[h]
             nc.scalar.activation(run[:, lo : lo + PASS], x_win[h][:].indirect(x_list[:, a * COLS : (a + 1) * COLS]), ACT.Copy)
-            step = keep.tile([P, PACK, P], F32, name=f"x_step{h}{a}", tag=f"stage{1 - h}" if a == 1 else f"x_step{h}", align_bytes=64)
-            bank = psum.tile([P, PACK, P], F32, name=f"x_bank{h}{a}", tag="x_bank", bufs=3)
+            if (h, a) == (0, 1):
+                step = keep.tile([P, PACK, P], F32, name="x_step01", tag="inv0")
+            elif (h, a) == (1, 1):
+                step = keep.tile([P, PACK, P], F32, name="x_step11", tag="g_woven1", align_bytes=64)
+            else:
+                step = keep.tile([P, PACK, P], F32, name=f"x_step{h}{a}")
+            bank = psum.tile([P, PACK, P], F32, name=f"x_bank{h}{a}", tag="g_bank00" if (h, a) == (1, 0) else f"x_bank{h}{a}")
             if a == 0:
-                nc.gpsimd.tensor_scalar(
-                    step[:], run[:, lo - 1 : lo - 1 + PASS].rearrange("p (q t) -> p t q", t=PACK), -0.6, 0.0, ALU.mult, ALU.add
+                nc.scalar.activation(
+                    step[:].rearrange("p t q -> p q t"),
+                    run[:, lo - 1 : lo - 1 + PASS].rearrange("p (q t) -> p q t", t=PACK),
+                    ACT.Copy,
+                    scale=-0.6,
                 )
                 for t in range(PACK):
                     nc.tensor.matmul(bank[:, t, :], run[:, lo + t : lo + PASS : PACK], ident[:], start=(t == 0), stop=False, is_transpose=True)
@@ -203,14 +220,17 @@ def tile_list_moment_steps_sized_shares_kernel(tc, xf, ra, gt, cb, bn, offs, off
         g_gather_turn(0, 0)
         g_gather_turn(1, 1)
         g_gather_turn(1, 0)
+        turn_weights()
         g_measure(0, 1)
         g_measure(0, 0)
         g_measure(1, 1)
-        g_finish(1)
+        g_weigh(1)
         g_measure(1, 0)
-        g_finish(0)
+        g_weigh(0)
+        g_finish(1)
         x_gather_turn(0, 0)
         x_gather_turn(0, 1)
+        g_finish(0)
         x_finish(0, 0)
         x_gather_turn(1, 0)
         x_gather_turn(1, 1)

from contextlib import ExitStack

import concourse.mybir as mybir
from concourse.masks import make_identity

K, J, N, T, V = 256, 1024, 256, 2048, 2048
FLOPS = 2 * K * J * N

F32 = mybir.dt.float32
BF16 = mybir.dt.bfloat16
U32 = mybir.dt.uint32
U16 = mybir.dt.uint16
U8 = mybir.dt.uint8
E4M3 = mybir.dt.float8_e4m3fn_x4
E5M2 = mybir.dt.float8_e5m2_x4
ALU = mybir.AluOpType
ACT = mybir.ActivationFunctionType
AX = mybir.AxisListType

P = 128
PACK = 4
RUN = 8
PASS = P * PACK
PASSES = J // PASS
COLS = PASS // 16
PAD = 8


def tile_list_moment_steps_sized_shares_kernel(tc, xf, ra, gt, cb, bn, offs, offs2, out):
    nc = tc.nc
    with ExitStack() as ctx:
        keep = ctx.enter_context(tc.tile_pool(name="keep", bufs=1))
        psum = ctx.enter_context(tc.psum_pool(name="psum", bufs=1))

        x_list = keep.tile([P, J // 16], U16, name="x_list")
        g_list = keep.tile([P, J // 16], U16, name="g_list")
        g_win = [keep.tile([P, V], F32, name=f"g_win{h}", tag=f"g_win{h}") for h in range(2)]
        x_win = [keep.tile([P, T], F32, name=f"x_win{h}") for h in range(2)]
        ra_0 = keep.tile([P, PACK], F32, name="ra_0")
        cb_0 = keep.tile([P, PACK], F32, name="cb_0")
        bn_col = keep.tile([P, 2], F32, name="bn_col")
        rows_1 = keep.tile([P, P], F32, name="rows_1")
        nc.vector.memset(rows_1[:], 0.0)

        nc.sync.dma_start(g_list[:], offs2)
        nc.sync.dma_start(g_win[0][:], gt[0:P, :])
        nc.scalar.dma_start(bn_col[:], bn.rearrange("o (p e) -> p (o e)", e=2))
        nc.sync.dma_start(g_win[1][:], gt[P : 2 * P, :])
        nc.sync.dma_start(x_list[:], offs)
        nc.sync.dma_start(cb_0[:], cb[0:PASS, :].rearrange("(p t) o -> p (t o)", t=PACK))
        nc.sync.dma_start(ra_0[:], ra[:, 0:PASS].rearrange("o (p t) -> p (o t)", t=PACK))
        nc.sync.dma_start(
            rows_1[0:PACK, :].rearrange("t (b r) -> t b r", r=RUN),
            ra[:, PASS:J].rearrange("o (b t r) -> t (o b) r", t=PACK, r=RUN),
        )
        nc.sync.dma_start(
            rows_1[PACK : 2 * PACK, :].rearrange("t (b r) -> t b r", r=RUN),
            cb[PASS:J, :].rearrange("(b t r) o -> t b (r o)", t=PACK, r=RUN),
        )
        nc.sync.dma_start(x_win[0][:], xf[0:P, :])
        nc.sync.dma_start(x_win[1][:], xf[P : 2 * P, :])

        ident = keep.tile([P, P], F32, name="ident")
        make_identity(nc, ident[:])

        x_run = [keep.tile([P, PAD + J], F32, name=f"x_run{h}") for h in range(2)]
        zero = keep.tile([P, 1], F32, name="zero")
        nc.vector.memset(zero[:], 0.0)
        for h in range(2):
            nc.scalar.activation(x_run[h][:, PAD - 1 : PAD], zero[:], ACT.Copy)

        head_bank = psum.tile([P, 2, P], F32, name="head_bank", tag="w")
        for e in range(2):
            nc.tensor.transpose(head_bank[:, e, :], bn_col[:, e : e + 1].to_broadcast([P, P]), ident[:])
        bn_rows = keep.tile([P, N], F32, name="bn_rows")
        nc.scalar.copy(bn_rows[:].rearrange("m (p e) -> m p e", e=2), head_bank[:].rearrange("m e p -> m p e"))
        weights_1 = keep.tile([P, 2 * PACK], F32, name="weights_1")
        ra_w = [ra_0[:], weights_1[:, 0:PACK]]
        cb_w = [cb_0[:], weights_1[:, PACK : 2 * PACK]]

        def turn_weights():
            bank = psum.tile([P, P], F32, name="weights_bank", tag="w")
            nc.tensor.transpose(bank[:], rows_1[:], ident[:])
            nc.vector.tensor_copy(weights_1[:], bank[:, 0 : 2 * PACK])

        g_bank = {}
        g_peak = {}
        first_turned = []

        def g_gather_turn(h, a):
            picked = keep.tile([P, PASS], F32, name=f"g_pick{h}{a}")
            window = g_win[h][:].indirect(g_list[:, a * COLS : (a + 1) * COLS])
            bank = psum.tile([P, PACK, P], F32, name=f"g_bank{h}{a}", tag=f"g_bank{h}{a}")
            if a == 1:
                nc.vector.tensor_copy(picked[:].rearrange("p (t b r) -> p b t r", t=PACK, r=RUN), window)
                for t in range(PACK):
                    nc.tensor.transpose(bank[:, t, :], picked[:, t * P : (t + 1) * P], ident[:])
            else:
                nc.scalar.activation(picked[:], window, ACT.Copy)
                for t in range(PACK):
                    nc.tensor.transpose(bank[:, t, :], picked[:, t:PASS:PACK], ident[:])
            g_bank[h, a] = bank

        def g_measure(h, a):
            if h == 0:
                if not first_turned:
                    first_turned.append(keep.tile([P, PASSES, PACK, P], F32, name="g_turn0", tag="g_win1"))
                turned = first_turned[0][:, a]
            else:
                turned = keep.tile([P, PACK, P], F32, name=f"g_turn{h}{a}")[:]
            nc.scalar.copy(turned, g_bank[h, a][:])
            peak = keep.tile([P, PACK], F32, name=f"g_peak{h}{a}")
            nc.vector.tensor_reduce(peak[:], turned, AX.X, ALU.max, apply_absolute_value=True)
            if h == 0:
                nc.vector.tensor_scalar_add(peak[:], peak[:], 0.2)
            g_peak[h, a] = peak

        g_codes = {}
        g_scales = {}

        g_factor = {}

        def g_weigh(a):
            den = keep.tile([P, PACK], F32, name=f"den{a}")
            nc.vector.scalar_tensor_tensor(den[:], g_peak[1, a][:], 0.2, g_peak[0, a][:], ALU.add, ALU.max)
            inv = keep.tile([P, PACK], F32, name=f"inv{a}", tag=f"inv{a}")
            nc.vector.reciprocal(inv[:], den[:])
            factor = keep.tile([P, PACK], F32, name=f"factor{a}")
            nc.vector.tensor_tensor(factor[:], inv[:], cb_w[a], ALU.mult)
            g_factor[a] = factor

        def g_finish(a):
            factor = g_factor[a]
            woven = keep.tile([P, N, PACK], BF16, name=f"g_woven{a}", tag=f"g_woven{a}", align_bytes=64)
            for h in range(2):
                nc.vector.tensor_tensor(
                    woven[:, h * P : (h + 1) * P, :],
                    g_bank[h, a][:].rearrange("p t n -> p n t"),
                    factor[:].unsqueeze(1).to_broadcast([P, P, PACK]),
                    ALU.mult,
                )
            g_codes[a] = keep.tile([P, N], U32, name=f"g_codes{a}", align_bytes=64)
            g_scales[a] = keep.tile([P, N], U8, name=f"g_scales{a}", align_bytes=64)
            nc.vector.quantize_mx(g_codes[a][:].bitcast(E5M2), g_scales[a][:], woven[:].rearrange("p n t -> p (n t)"))

        u_codes = {}
        u_scales = {}
        x_bank = {}

        def x_gather_turn(h, a):
            lo = PAD + a * PASS
            run = x_run[h]
            nc.scalar.activation(run[:, lo : lo + PASS], x_win[h][:].indirect(x_list[:, a * COLS : (a + 1) * COLS]), ACT.Copy)
            if (h, a) == (0, 1):
                step = keep.tile([P, PACK, P], F32, name="x_step01", tag="inv0")
            elif (h, a) == (1, 1):
                step = keep.tile([P, PACK, P], F32, name="x_step11", tag="g_woven1", align_bytes=64)
            else:
                step = keep.tile([P, PACK, P], F32, name=f"x_step{h}{a}")
            bank = psum.tile([P, PACK, P], F32, name=f"x_bank{h}{a}", tag="g_bank00" if (h, a) == (1, 0) else f"x_bank{h}{a}")
            if a == 0:
                nc.scalar.activation(
                    step[:].rearrange("p t q -> p q t"),
                    run[:, lo - 1 : lo - 1 + PASS].rearrange("p (q t) -> p q t", t=PACK),
                    ACT.Copy,
                    scale=-0.6,
                )
                for t in range(PACK):
                    nc.tensor.matmul(bank[:, t, :], run[:, lo + t : lo + PASS : PACK], ident[:], start=(t == 0), stop=False, is_transpose=True)
                for t in range(PACK):
                    nc.tensor.matmul(bank[:, t, :], step[:, t, :], ident[:], start=False, stop=(t == PACK - 1), is_transpose=True)
            else:
                before = run[:, lo - 1 : lo - 1 + PASS].rearrange("p (b t r) -> p t b r", t=PACK, r=RUN)
                here = run[:, lo : lo + PASS].rearrange("p (b t r) -> p t b r", t=PACK, r=RUN)
                for t in range(PACK):
                    nc.vector.scalar_tensor_tensor(
                        step[:, t, :].rearrange("p (b r) -> p b r", r=RUN), before[:, t], -0.6, here[:, t], ALU.mult, ALU.add
                    )
                    nc.tensor.transpose(bank[:, t, :], step[:, t, :], ident[:])
            x_bank[h, a] = bank

        def x_finish(h, a):
            woven = keep.tile([P, P, PACK], BF16, name=f"u_woven{h}{a}", align_bytes=64)
            nc.vector.tensor_tensor(
                woven[:],
                x_bank[h, a][:].rearrange("p t k -> p k t"),
                ra_w[a].unsqueeze(1).to_broadcast([P, P, PACK]),
                ALU.mult,
            )
            u_codes[h, a] = keep.tile([P, P], U32, name=f"u_codes{h}{a}", align_bytes=64)
            u_scales[h, a] = keep.tile([P, P], U8, name=f"u_scales{h}{a}", align_bytes=64)
            nc.vector.quantize_mx(u_codes[h, a][:].bitcast(E4M3), u_scales[h, a][:], woven[:].rearrange("p k t -> p (k t)"))

        def shares(h):
            moment = psum.tile([P, N], F32, name=f"moment{h}", tag="w")
            for a in range(PASSES):
                nc.tensor.matmul_mx(
                    out=moment[:],
                    lhsT=u_codes[h, a][:].bitcast(E4M3),
                    lhsT_scale=u_scales[h, a][:],
                    rhs=g_codes[a][:].bitcast(E5M2),
                    rhs_scale=g_scales[a][:],
                    start=(a == 0),
                    stop=(a == PASSES - 1),
                )
            minus_z = keep.tile([P, N], F32, name=f"minus_z{h}")
            nc.vector.scalar_tensor_tensor(minus_z[:], moment[:], -0.02, bn_rows[:], ALU.mult, ALU.subtract)
            low = keep.tile([P, 1], F32, name=f"low{h}")
            nc.vector.tensor_reduce(low[:], minus_z[:], AX.X, ALU.min)
            ew = keep.tile([P, N], F32, name=f"ew{h}")
            total = keep.tile([P, 1], F32, name=f"total{h}")
            nc.scalar.activation(ew[:], minus_z[:], ACT.Exp, bias=low[:], scale=-1.0, accum_out=total[:])
            inv_total = keep.tile([P, 1], F32, name=f"inv_total{h}")
            nc.vector.reciprocal(inv_total[:], total[:])
            result = keep.tile([P, N], F32, name=f"result{h}")
            nc.vector.tensor_scalar(result[:], ew[:], inv_total[:], 256.0, ALU.mult, ALU.mult)
            nc.sync.dma_start(out[h * P : (h + 1) * P, :], result[:])

        g_gather_turn(0, 1)
        g_gather_turn(0, 0)
        g_gather_turn(1, 1)
        g_gather_turn(1, 0)
        turn_weights()
        g_measure(0, 1)
        g_measure(0, 0)
        g_measure(1, 1)
        g_weigh(1)
        g_measure(1, 0)
        g_weigh(0)
        g_finish(1)
        x_gather_turn(0, 0)
        x_gather_turn(0, 1)
        g_finish(0)
        x_finish(0, 0)
        x_gather_turn(1, 0)
        x_gather_turn(1, 1)
        x_finish(0, 1)
        x_finish(1, 0)
        x_finish(1, 1)
        shares(0)
        shares(1)
